import numpy as np, ml_dtypes
CORES = [52,68,84,180,196,212,308,324,340]
N = 9
F = 128
def setup_inputs(rng):
    return {"a": rng.standard_normal((N, 128, 128), dtype=np.float32).astype(ml_dtypes.bfloat16), "w": rng.standard_normal((N, 128, F), dtype=np.float32).astype(ml_dtypes.bfloat16)}
def setup_inputs_big(rng):
    d = setup_inputs(rng)
    for k in ("a", "w"): d[k] = (d[k].astype(np.float32) * 1024.0).astype(d[k].dtype)
    return d
def setup_inputs_small(rng):
    d = setup_inputs(rng)
    for k in ("a", "w"): d[k] = (d[k].astype(np.float32) * (1 / 1024.0)).astype(d[k].dtype)
    return d
def setup_inputs_apart(rng):
    d = setup_inputs(rng)
    f = (10.0 ** rng.permutation(np.linspace(-1.5, 1.5, N))).astype(np.float32).reshape(N, 1, 1)
    for k in ("a", "w"): d[k] = (d[k].astype(np.float32) * f).astype(d[k].dtype)
    return d
def setup_inputs_neg(rng):
    d = setup_inputs(rng)
    d["a"] = (np.abs(d["a"].astype(np.float32)) * 1048576.0).astype(d["a"].dtype); d["w"] = (-np.abs(d["w"].astype(np.float32))).astype(d["w"].dtype)
    return d
def reference(a, w):
    A, W = a.astype(np.float64), w.astype(np.float64)
    p = np.stack([A[j].T @ W[j] for j in range(N)])
    return {"y": np.maximum.accumulate(p, axis=0).astype(ml_dtypes.bfloat16)}

from concourse.bass import DstId, RemoteDMATransfer
from concourse.mybir import AluOpType

N = 9
F = 128
SLOTS = 5

SCRATCH = {
    "a_sb": ("sbuf", [128, 128], "bfloat16"),
    "w_sb": ("sbuf", [128, F], "bfloat16"),
    "p_sb": ("sbuf", [128, F], "bfloat16"),
    "m_sb": ("sbuf", [128, F], "bfloat16"),
    "y_sb": ("sbuf", [128, F], "bfloat16"),
    "land": ("sbuf", [128, SLOTS * F], "bfloat16"),
    "ps": ("psum", [128, F], "float32"),
    "acc_m": ("psum", [128, F], "float32"),
    "acc_y": ("psum", [128, F], "float32"),
}
SEMAPHORES = (["arr%d" % j for j in range(N - 1)] +
              ["arr_m", "loaded", "mm", "pready", "vch", "mready", "yready", "sent_a", "sent_b", "sent_m", "stored"])


def _plan(cores, topo):
    n = len(cores)

    def ok(j, r):
        return topo.may_write(cores[j], cores[r])

    far = [r for r in range(n) if not all(ok(j, r) for j in range(r))]
    head = list(range(far[0]))
    relay_of = {}
    for f in far:
        relay_of[f] = [q for q in head
                       if ok(q, f) and topo.chip(cores[q]) == topo.chip(cores[f])
                       and topo.rack(topo.host(cores[q])) != topo.rack(topo.host(cores[f]))
                       and all(ok(j, q) for j in head if j != q)][0]
    relays = sorted(set(relay_of.values()))
    waves = {}
    for j in range(n):
        k = j % len(relays)
        w1 = [q for q in relays[k:] + relays[:k] if q != j] if j in head else []
        w2 = [r for r in range(j + 1, n) if r not in w1 and ((j in head) == (r in head))]
        waves[j] = (w1, w2)
    inbound = {}
    for r in range(n):
        src = [j for j in range(n) if r in waves[j][0] + waves[j][1]]
        inbound[r] = sorted(src, key=lambda j: ((waves[j][0] + waves[j][1]).index(r), j))
    return relay_of, waves, inbound


def rank_program(g, core, T, topo):
    rank = T.rank_of(core)
    if rank is None:
        return
    cores = list(T.cores)
    relay_of, waves, inbound = _plan(cores, topo)
    sem, v = T.sem, g.vector
    wave1, wave2 = waves[rank]
    my_far = [f for f in relay_of if relay_of[f] == rank]
    tiles = inbound[rank]
    gets_m = rank in relay_of

    def slot(r, tag):
        s = len(inbound[r]) if tag == "m" else inbound[r].index(tag)
        return T.land[:, s * F:(s + 1) * F]

    def engines(dst):
        m = topo.mask(core, cores[dst])
        return m, bin(m).count("1")

    g.sync.dma_start(T.a_sb[:], T.a[:]).then_inc(sem.loaded, 16)
    g.scalar.dma_start(T.w_sb[:], T.w[:]).then_inc(sem.loaded, 16)
    g.tensor.wait_ge(sem.loaded, 32)
    g.tensor.matmul(T.ps[:], T.a_sb[:], T.w_sb[:], True, True).then_inc(sem.mm, 1)
    v.wait_ge(sem.mm, 1)
    sends = bool(wave1 or wave2)
    if sends or not tiles:
        v.tensor_copy(T.p_sb[:], T.ps[:]).then_inc(sem.pready, 1)

    def send(src, dsts, tag, remote_sem, local_sem):
        m, k = engines(dsts[0])
        ids = [topo.addr(cores[d], core) for d in dsts]
        if len(dsts) == 1:
            g.remote_dma(slot(dsts[0], tag), src[:], remote_sem, local_sem, ids[0][1], ids[0][0], m)
        else:
            g.remote_dma_fused([RemoteDMATransfer(dst_ids=[DstId(rid=a, pnc=p) for a, p in ids], dma_engine_mask=m,
                                                  remote_sem=remote_sem, srcs=[src[:]],
                                                  dsts=[slot(d, tag) for d in dsts], alu_op=0)], local_sem=local_sem)
        return k

    left = []
    if sends:
        g.wait_ge(sem.pready, 1)
        if wave1:
            left.append((sem.sent_a, send(T.p_sb, wave1, rank, sem["arr%d" % rank], sem.sent_a)))
        if wave2:
            left.append((sem.sent_b, send(T.p_sb, wave2, rank, sem["arr%d" % rank], sem.sent_b)))
    if my_far:
        g.wait_ge(sem.mready, 1)
        left.append((sem.sent_m, send(T.m_sb, my_far, "m", sem.arr_m, sem.sent_m)))
    for s, k in left:
        g.wait_ge(s, k)

    nv = [0]
    seen = set()

    def chain(tags, acc, out, done):
        cur = T.ps
        for i, t in enumerate(tags):
            if t not in seen:
                seen.add(t)
                src_rank = relay_of[rank] if t == "m" else t
                k = bin(topo.mask(cores[src_rank], core)).count("1")
                v.wait_ge(sem.arr_m if t == "m" else sem["arr%d" % t], k)
            if i:
                v.wait_ge(sem.vch, nv[0])
            if i == len(tags) - 1:
                v.tensor_tensor(out[:], cur[:], slot(rank, t), AluOpType.max).then_inc(done, 1)
            else:
                v.tensor_tensor(acc[:], cur[:], slot(rank, t), AluOpType.max).then_inc(sem.vch, 1)
                nv[0] += 1
            cur = acc

    y_src, y_sem, hold = T.y_sb, sem.yready, None
    if my_far:
        chain(tiles, T.acc_m, T.m_sb, sem.mready)
        hold = left[-1]
        mine = [t for t in tiles if t < rank]
        if len(mine) == len(tiles):
            y_src, y_sem = T.m_sb, sem.mready
        else:
            chain(mine, T.acc_y, T.y_sb, sem.yready)
    elif tiles or gets_m:
        chain(tiles + (["m"] if gets_m else []), T.acc_y, T.y_sb, sem.yready)
    else:
        y_src, y_sem = T.p_sb, sem.pready
        hold = left[0] if wave1 else None

    g.sync.wait_ge(y_sem, 1)
    if hold:
        g.sync.wait_ge(hold[0], hold[1])
    g.sync.dma_start(T.y[:], y_src[:]).then_inc(sem.stored, 16)
    g.sync.wait_ge(sem.stored, 16)
